import numpy as np
import ml_dtypes


def mxq(x, axis, fmt="e4m3"):
    dtype, down = {"e4m3": (ml_dtypes.float8_e4m3fn, 7), "e5m2": (ml_dtypes.float8_e5m2, 14)}[fmt]
    v = np.moveaxis(np.asarray(x, np.float32).astype(ml_dtypes.bfloat16).astype(np.float64), axis, -1)
    blocks = v.reshape(v.shape[:-1] + (-1, 32))
    amax = np.abs(blocks).max(-1, keepdims=True)
    byte = np.maximum(np.where(amax > 0, np.frexp(amax)[1] - 1 + 127, 0) - down, 1)
    scale = np.exp2(byte - 127.0)
    codes = (blocks / scale).astype(np.float32).astype(dtype).astype(np.float64)
    return np.moveaxis((codes * scale).reshape(v.shape), -1, axis)


WIDE = False


def mx_kscale(k):
    if not WIDE:
        return np.ones(k)
    levels = np.array([10, -10, 5, -5, 0])
    if k % 512:
        return np.exp2(np.random.permutation(np.resize(levels, k // 32))).repeat(32)
    a = np.empty((k // 512, 16))
    for p in range(k // 512):
        a[p, :8] = np.random.permutation(np.resize(levels, 8))
        for g in range(8):
            far = levels[np.abs(levels - a[p, g]) >= 10]
            a[p, g + 8] = far[np.random.randint(len(far))]
    return np.exp2(a.ravel()).repeat(32)


def f64(x):
    return np.asarray(x).astype(np.float64)


def striped(idx):
    return np.tile(np.asarray(idx).reshape(-1, 16).T, (8, 1)).astype(np.uint16)


def unstriped(offs):
    return offs[:16].T.reshape(-1).astype(np.int64)


E2M1 = np.array([0.0, 0.5, 1.0, 1.5, 2.0, 3.0, 4.0, 6.0, -0.0, -0.5, -1.0, -1.5, -2.0, -3.0, -4.0, -6.0])


def pack_weight(w, fmt):
    k, n = w.shape
    w = f64(np.asarray(w, np.float32).astype(ml_dtypes.bfloat16)).reshape(k // 32, 32, n)
    amax = np.abs(w).max(1)
    if fmt == "e4m3":
        byte = np.frexp(amax)[1] - 1 + 127 - 7
    else:
        mant, ex = np.frexp(amax / 6.0)
        byte = np.where(mant > 0.5, ex, ex - 1) + 127
    byte = np.clip(np.where(amax > 0, byte, 1), 1, 254)
    scaled = (w * np.exp2(127.0 - byte)[:, None, :]).reshape(k, n).astype(np.float32)
    by_word = np.ascontiguousarray(scaled.reshape(k // 512, 128, 4, n).transpose(0, 1, 3, 2))
    if fmt == "e4m3":
        words = by_word.astype(ml_dtypes.float8_e4m3fn).view(np.uint8)
    else:
        c = by_word.astype(ml_dtypes.float4_e2m1fn).view(np.uint8) & 0xF
        words = (c[..., 0::2] | (c[..., 1::2] << 4)).reshape(k // 512, 128, 2 * n)
    return np.ascontiguousarray(words), np.ascontiguousarray(byte.astype(np.uint8).reshape(k // 512, 16, n))


def unpack_weight(words, scales, fmt):
    g, _, n = scales.shape
    words = np.ascontiguousarray(words).reshape(g, 128, n, -1)
    if fmt == "e4m3":
        vals = words.view(ml_dtypes.float8_e4m3fn).astype(np.float64)
    else:
        nib = np.empty((g, 128, n, 4), np.uint8)
        nib[..., 0::2] = words & 0xF
        nib[..., 1::2] = words >> 4
        vals = E2M1[nib]
    vals = vals * np.repeat(np.exp2(scales.astype(np.float64) - 127.0), 8, axis=1)[..., None]
    return vals.transpose(0, 1, 3, 2).reshape(g * 512, n)


D, E, T, I, Q = 512, 512, 2048, 512, 128


def setup_inputs():
    n = np.random.standard_normal
    idx = np.random.permutation(T)[:I]
    fd = mx_kscale(D)
    fe = mx_kscale(E)
    keysp = pack_weight(n((D, T)) / fd[:, None], "e2m1")
    valsp = pack_weight(n((E, T)) / fe[:, None], "e2m1")
    return {
        "query": (n((D, Q)) * 0.8 / np.sqrt(D) * fd[:, None]).astype(np.float32),
        "query2": (n((D, Q)) * 0.8 / np.sqrt(D) * fd[:, None]).astype(np.float32),
        "query3": (n((D, Q)) * 0.8 / np.sqrt(D) * fd[:, None]).astype(np.float32),
        "keys_words": keysp[0],
        "keys_scales": keysp[1],
        "gout": (n((E, Q)) * 1 / np.sqrt(E) * fe[:, None]).astype(np.float32),
        "vals_words": valsp[0],
        "vals_scales": valsp[1],
        "size": (np.random.uniform(0.5, 2.0, (1, I))).astype(np.float32),
        "dquery": (n((D, Q)) * 1.0 / np.sqrt(D) * fd[:, None]).astype(np.float32),
        "base": (0.5 * n((Q, I))).astype(np.float32),
        "offs": striped(idx),
    }


def reference(query, query2, query3, keys_words, keys_scales, gout, vals_words, vals_scales, size, dquery, base, offs):
    idx = unstriped(offs)
    keysu = unpack_weight(keys_words, keys_scales, "e2m1")
    valsu = unpack_weight(vals_words, vals_scales, "e2m1")
    queryq = mxq(f64(query), 0, "e4m3")
    keysidxg = keysu[:, idx]
    a = queryq.T @ keysidxg
    dqueryq = mxq(f64(dquery), 0, "e4m3")
    ta = dqueryq.T @ keysidxg
    query2q = mxq(f64(query2), 0, "e4m3")
    b = query2q.T @ keysidxg
    query3q = mxq(f64(query3), 0, "e4m3")
    h1 = query3q.T @ keysidxg
    s = np.log(np.exp(a) + np.exp(b) + np.exp(h1))
    p = np.exp(s - np.max(s, axis=1, keepdims=True))
    z = np.sum(p, axis=1, keepdims=True)
    goutq = mxq(f64(gout), 0, "e4m3")
    valsidxg = valsu[:, idx]
    c0 = goutq.T @ valsidxg
    dz = np.sum(c0 * p * f64(size) / np.square(z) * (-1.0), axis=1, keepdims=True)
    dp = c0 / z * f64(size) + dz
    ds = dp * p
    xs = ta * np.exp(a) / (np.exp(a) + np.exp(b) + np.exp(h1))
    xp = xs * p
    xz = np.sum(xp, axis=1, keepdims=True)
    xdz = np.sum((xp * f64(size) * c0 - xz * z * 2.0 * c0 * p * f64(size) / np.square(z)) / np.square(z) * (-1.0), axis=1, keepdims=True)
    xdp = xz * c0 / np.square(z) * (-1.0) * f64(size) + xdz
    xds = xdp * p + xp * dp
    xda = (xds - ta * np.exp(a) * ds / (np.exp(a) + np.exp(b) + np.exp(h1))) / (np.exp(a) + np.exp(b) + np.exp(h1)) * np.exp(a) + ta * np.exp(a) * ds / (np.exp(a) + np.exp(b) + np.exp(h1))
    y = xda * 512.0 + f64(base)
    return y

@@ -1,0 +1,186 @@
+from contextlib import ExitStack
+
+import concourse.mybir as mybir
+
+D, E, T, I, Q = 512, 512, 2048, 512, 128
+FLOPS = 5 * 2 * D * Q * I
+
+F32 = mybir.dt.float32
+BF16 = mybir.dt.bfloat16
+I32 = mybir.dt.int32
+U32 = mybir.dt.uint32
+U16 = mybir.dt.uint16
+U8 = mybir.dt.uint8
+FP8X4 = mybir.dt.float8_e4m3fn_x4
+FP4X4 = mybir.dt.float4_e2m1fn_x4
+ALU = mybir.AluOpType
+ACT = mybir.ActivationFunctionType
+AX = mybir.AxisListType
+
+P = 128
+PACK = 4
+OUT_SCALE = 512.0
+
+
+def tile_attend_hvcommittee_kernel(tc, query, query2, query3, keys_words, keys_scales, gout, vals_words, vals_scales, size, dquery, base, offs, out):
+    nc = tc.nc
+    with ExitStack() as ctx:
+        sb = ctx.enter_context(tc.tile_pool(name="sb", bufs=1))
+        ps = ctx.enter_context(tc.psum_pool(name="ps", bufs=1))
+
+        offsets = sb.tile([P, I // 16], U16, name="offsets")
+        nc.sync.dma_start(offsets[:], offs)
+
+        def load_scale_rows(name, scales, pool, queue):
+            plane = pool.tile([P, T], U8, name=name, align_bytes=64)
+            nc.vector.memset(plane[:].bitcast(I32), 0)
+            for quad in range(4):
+                queue.dma_start(plane[32 * quad : 32 * quad + 4, :].bitcast(I32), scales[0, 4 * quad : 4 * quad + 4, :].bitcast(I32))
+            return plane
+
+        def load_words(name, words, pool):
+            pool_words = pool.tile([P, T], U16, name=name, tag=name, align_bytes=64)
+            nc.sync.dma_start(pool_words[:].bitcast(I32), words[0].bitcast(I32))
+            return pool_words
+
+        def load_rows(name, src):
+            raw = late.tile([P, PACK * Q], F32, name=name, align_bytes=64)
+            nc.sync.dma_start(raw[:], src.rearrange("(p t) q -> p (t q)", t=PACK))
+            return raw
+
+        def gather(name, window, dtype, tag=""):
+            picked = sb.tile([P, I], dtype, name=name, tag=tag, align_bytes=64)
+            nc.vector.tensor_copy(picked[:], window[:].indirect(offsets[:]))
+            return picked
+
+        def interleave(grouped, raw):
+            nc.scalar.activation(
+                grouped.rearrange("p (q t) -> p q t", t=PACK),
+                raw[:].rearrange("p (t q) -> p q t", t=PACK),
+                ACT.Copy,
+            )
+
+        def quantize(name, grouped, n, tag=""):
+            codes = sb.tile([P, n * Q], U32, name=name + "_codes", tag=tag, align_bytes=64)
+            scales = sb.tile([P, n * Q], U8, name=name + "_scales", align_bytes=64)
+            nc.vector.quantize_mx(out=codes[:].bitcast(FP8X4), scales=scales[:], in_=grouped[:])
+            return [(codes[:, m * Q : (m + 1) * Q], scales[:, m * Q : (m + 1) * Q]) for m in range(n)]
+
+        def product(name, rows, words, scales):
+            bank = ps.tile([Q, I], F32, name=name)
+            nc.tensor.matmul_mx(out=bank[:], lhsT=rows[0].bitcast(FP8X4), lhsT_scale=rows[1], rhs=words[:].bitcast(FP4X4), rhs_scale=scales[:], start=True, stop=True)
+            return bank
+
+        def wide(name):
+            return sb.tile([Q, I], F32, name=name, align_bytes=64)
+
+        def column(name, n=1):
+            return sb.tile([Q, n], F32, name=name)
+
+        size4 = sb.tile([P, PACK], F32, name="size4")
+        nc.sync.dma_start(size4[:], size[0].rearrange("(p j) -> p j", j=PACK))
+        kw_pool = load_words("kw_pool", keys_words, sb)
+        ks_pool = load_scale_rows("ks_pool", keys_scales, sb, nc.sync)
+
+        ident = sb.tile([P, P], F32, name="ident")
+        with tc.tile_pool(name="early", bufs=1) as early:
+            zeros = early.tile([P, 4608], F32, name="zeros", align_bytes=64)
+            nc.gpsimd.memset(zeros[:, :P], 0.0)
+            nc.gpsimd.affine_select(out=ident[:], in_=zeros[:, :P], compare_op=ALU.not_equal, fill=1.0, base=0, pattern=[[-1, P]], channel_multiplier=1)
+        late = ctx.enter_context(tc.tile_pool(name="late", bufs=1))
+
+        q1_raw = load_rows("q1_raw", query)
+        q2_raw = load_rows("q2_raw", query2)
+        q3_raw = load_rows("q3_raw", query3)
+        dq_raw = load_rows("dq_raw", dquery)
+        go_raw = load_rows("go_raw", gout)
+        vs_pool = load_scale_rows("vs_pool", vals_scales, sb, nc.gpsimd)
+        vw_pool = load_words("vw_pool", vals_words, late)
+        base_sb = late.tile([Q, I], F32, name="base_sb", align_bytes=64)
+        nc.sync.dma_start(base_sb[:], base)
+
+        kw = gather("kw", kw_pool, U16)
+        ks = gather("ks", ks_pool, U8)
+
+        banks = []
+        for name, raw in (("a", q1_raw), ("b", q2_raw), ("h", q3_raw)):
+            grouped = sb.tile([P, Q * PACK], BF16, name=name + "_bf", align_bytes=64)
+            interleave(grouped[:], raw)
+            banks.append(product(name, quantize(name, grouped, 1)[0], kw, ks))
+        a, b, h = banks
+        dq_go = sb.tile([P, 2 * Q * PACK], BF16, name="dq_go", align_bytes=64)
+        interleave(dq_go[:, : Q * PACK], dq_raw)
+        interleave(dq_go[:, Q * PACK :], go_raw)
+
+        size_ps = ps.tile([P, PACK, P], F32, name="size_ps")
+        for j in range(PACK):
+            nc.tensor.transpose(size_ps[:, j, :], size4[:, j : j + 1].to_broadcast([P, P]), ident[:])
+
+        neg_maxes = []
+        for n, bank in enumerate((a, b, h)):
+            part = sb.tile([Q, 1], F32, name="neg_max%d" % n, tag="after_max%d" % n, align_bytes=64)
+            nc.vector.tensor_reduce(part[:], bank[:], AX.X, ALU.max, negate=True)
+            neg_maxes.append(part)
+        neg_max = sb.tile([Q, 1], F32, name="neg_max", tag="after_exp", align_bytes=64)
+        nc.vector.tensor_scalar(neg_max[:], neg_maxes[0][:], neg_maxes[1][:], neg_maxes[2][:], ALU.min, ALU.min)
+
+        dq_q, go_q = quantize("dq_go", dq_go, 2, tag="after_max2")
+        ta = product("ta", dq_q, kw, ks)
+        vs = gather("vs", vs_pool, U8, tag="after_max0")
+        vw = gather("vw", vw_pool, U16, tag="after_max1")
+        c0 = product("c0", go_q, vw, vs)
+
+        z3 = column("z3", 3)
+        exps = []
+        for n, bank in enumerate((a, b, h)):
+            e = wide("exp%d" % n)
+            nc.scalar.activation(e[:], bank[:], ACT.Exp, bias=neg_max[:], accum_out=z3[:, n : n + 1])
+            exps.append(e)
+        ea, eb, eh = exps
+        z3n = column("z3n", 3)
+        neg_z = column("neg_z")
+        nc.scalar.activation(z3n[:], z3[:], ACT.Identity, scale=-1.0, accum_out=neg_z[:])
+
+        size_row = sb.tile([Q, I], F32, name="size_row", tag="after_exp", align_bytes=64)
+        nc.scalar.copy(size_row[:].rearrange("p (s j) -> p s j", j=PACK), size_ps[:].rearrange("p j s -> p s j"))
+
+        x = late.tile([Q, I], F32, name="x", tag="vw_pool", align_bytes=64)
+        sum_x = column("sum_x")
+        nc.vector.scalar_tensor_tensor(x[:], ta[:], 1.0, ea[:], ALU.mult, ALU.mult, accum_out=sum_x[:])
+        g = wide("g")
+        nc.vector.tensor_tensor(g[:], c0[:], size_row[:], ALU.mult)
+        neg_rz = column("neg_rz")
+        nc.vector.reciprocal(neg_rz[:], neg_z[:])
+        t3 = column("t3", 3)
+        for n, e in enumerate(exps):
+            eg = wide("eg%d" % n)
+            nc.vector.scalar_tensor_tensor(eg[:], e[:], 1.0, g[:], ALU.mult, ALU.mult, accum_out=t3[:, n : n + 1])
+        xg = wide("xg")
+        sum_xg = column("sum_xg")
+        nc.vector.scalar_tensor_tensor(xg[:], x[:], 1.0, g[:], ALU.mult, ALU.mult, accum_out=sum_xg[:])
+
+        neg_xb = column("neg_xb")
+        nc.scalar.activation(neg_xb[:], sum_x[:], ACT.Identity, scale=neg_rz[:])
+        dta = wide("dta")
+        nc.scalar.activation(dta[:], ta[:], ACT.Identity, bias=neg_xb[:])
+        k = column("k")
+        nc.scalar.activation(k[:], neg_rz[:], ACT.Identity, scale=-OUT_SCALE)
+        t3n = column("t3n", 3)
+        neg_mu = column("neg_mu")
+        nc.scalar.activation(t3n[:], t3[:], ACT.Identity, scale=neg_rz[:], accum_out=neg_mu[:])
+        xb_mu = column("xb_mu")
+        nc.scalar.activation(xb_mu[:], neg_mu[:], ACT.Identity, scale=neg_xb[:])
+        neg_c = column("neg_c")
+        nc.scalar.activation(neg_c[:], sum_xg[:], ACT.Identity, scale=neg_rz[:], bias=xb_mu[:])
+
+        halves = [slice(0, I // 2), slice(I // 2, I)]
+        u = [sb.tile([Q, I // 2], F32, name="u%d" % n, align_bytes=64) for n in range(2)]
+        v = [sb.tile([Q, I // 2], F32, name="v%d" % n, align_bytes=64) for n in range(2)]
+        y = [sb.tile([Q, I // 2], F32, name="y%d" % n, align_bytes=64) for n in range(2)]
+        for n, cols in enumerate(halves):
+            nc.vector.scalar_tensor_tensor(u[n][:], g[:, cols], neg_mu[:], dta[:, cols], ALU.add, ALU.mult)
+        for n, cols in enumerate(halves):
+            nc.vector.scalar_tensor_tensor(v[n][:], u[n][:], neg_c[:], ea[:, cols], ALU.add, ALU.mult)
+        for n, cols in enumerate(halves):
+            nc.vector.scalar_tensor_tensor(y[n][:], v[n][:], k[:], base_sb[:, cols], ALU.mult, ALU.add)
+            nc.sync.dma_start(out[:, cols], y[n][:])

@@ -1,6 +1,7 @@
 from contextlib import ExitStack
 
 import concourse.mybir as mybir
+from concourse.masks import make_identity
 
 D, E, T, I, Q = 512, 512, 2048, 512, 128
 FLOPS = 5 * 2 * D * Q * I
@@ -31,25 +32,25 @@ def tile_attend_hvcommittee_kernel(tc, query, query2, query3, keys_words, keys_s
         offsets = sb.tile([P, I // 16], U16, name="offsets")
         nc.sync.dma_start(offsets[:], offs)
 
-        def load_scale_rows(name, scales, pool, queue):
-            plane = pool.tile([P, T], U8, name=name, align_bytes=64)
+        def load_scale_rows(name, scales):
+            plane = sb.tile([P, T], U8, name=name, align_bytes=64)
             nc.vector.memset(plane[:].bitcast(I32), 0)
             for quad in range(4):
-                queue.dma_start(plane[32 * quad : 32 * quad + 4, :].bitcast(I32), scales[0, 4 * quad : 4 * quad + 4, :].bitcast(I32))
+                nc.sync.dma_start(plane[32 * quad : 32 * quad + 4, :].bitcast(I32), scales[0, 4 * quad : 4 * quad + 4, :].bitcast(I32))
             return plane
 
-        def load_words(name, words, pool):
-            pool_words = pool.tile([P, T], U16, name=name, tag=name, align_bytes=64)
+        def load_words(name, words):
+            pool_words = sb.tile([P, T], U16, name=name, align_bytes=64)
             nc.sync.dma_start(pool_words[:].bitcast(I32), words[0].bitcast(I32))
             return pool_words
 
         def load_rows(name, src):
-            raw = late.tile([P, PACK * Q], F32, name=name, align_bytes=64)
+            raw = sb.tile([P, PACK * Q], F32, name=name, align_bytes=64)
             nc.sync.dma_start(raw[:], src.rearrange("(p t) q -> p (t q)", t=PACK))
             return raw
 
-        def gather(name, window, dtype, tag=""):
-            picked = sb.tile([P, I], dtype, name=name, tag=tag, align_bytes=64)
+        def gather(name, window, dtype):
+            picked = sb.tile([P, I], dtype, name=name, align_bytes=64)
             nc.vector.tensor_copy(picked[:], window[:].indirect(offsets[:]))
             return picked
 
@@ -60,8 +61,8 @@ def tile_attend_hvcommittee_kernel(tc, query, query2, query3, keys_words, keys_s
                 ACT.Copy,
             )
 
-        def quantize(name, grouped, n, tag=""):
-            codes = sb.tile([P, n * Q], U32, name=name + "_codes", tag=tag, align_bytes=64)
+        def quantize(name, grouped, n):
+            codes = sb.tile([P, n * Q], U32, name=name + "_codes", align_bytes=64)
             scales = sb.tile([P, n * Q], U8, name=name + "_scales", align_bytes=64)
             nc.vector.quantize_mx(out=codes[:].bitcast(FP8X4), scales=scales[:], in_=grouped[:])
             return [(codes[:, m * Q : (m + 1) * Q], scales[:, m * Q : (m + 1) * Q]) for m in range(n)]
@@ -77,27 +78,24 @@ def tile_attend_hvcommittee_kernel(tc, query, query2, query3, keys_words, keys_s
         def column(name, n=1):
             return sb.tile([Q, n], F32, name=name)
 
-        size4 = sb.tile([P, PACK], F32, name="size4")
-        nc.sync.dma_start(size4[:], size[0].rearrange("(p j) -> p j", j=PACK))
-        kw_pool = load_words("kw_pool", keys_words, sb)
-        ks_pool = load_scale_rows("ks_pool", keys_scales, sb, nc.sync)
-
-        ident = sb.tile([P, P], F32, name="ident")
-        with tc.tile_pool(name="early", bufs=1) as early:
-            zeros = early.tile([P, 4608], F32, name="zeros", align_bytes=64)
-            nc.gpsimd.memset(zeros[:, :P], 0.0)
-            nc.gpsimd.affine_select(out=ident[:], in_=zeros[:, :P], compare_op=ALU.not_equal, fill=1.0, base=0, pattern=[[-1, P]], channel_multiplier=1)
-        late = ctx.enter_context(tc.tile_pool(name="late", bufs=1))
-
+        kw_pool = load_words("kw_pool", keys_words)
+        ks_pool = load_scale_rows("ks_pool", keys_scales)
         q1_raw = load_rows("q1_raw", query)
         q2_raw = load_rows("q2_raw", query2)
         q3_raw = load_rows("q3_raw", query3)
+        vs_pool = load_scale_rows("vs_pool", vals_scales)
+        vw_pool = load_words("vw_pool", vals_words)
         dq_raw = load_rows("dq_raw", dquery)
         go_raw = load_rows("go_raw", gout)
-        vs_pool = load_scale_rows("vs_pool", vals_scales, sb, nc.gpsimd)
-        vw_pool = load_words("vw_pool", vals_words, late)
-        base_sb = late.tile([Q, I], F32, name="base_sb", align_bytes=64)
+        size4 = sb.tile([P, PACK], F32, name="size4")
+        nc.sync.dma_start(size4[:], size[0].rearrange("(p j) -> p j", j=PACK))
+        base_sb = wide("base_sb")
         nc.sync.dma_start(base_sb[:], base)
+
+        ident = sb.tile([P, P], F32, name="ident")
+        make_identity(nc, ident[:])
+        warm = column("warm")
+        nc.scalar.activation(warm[:], ident[:, 0:1], ACT.Exp)
 
         kw = gather("kw", kw_pool, U16)
         ks = gather("ks", ks_pool, U8)
@@ -108,27 +106,26 @@ def tile_attend_hvcommittee_kernel(tc, query, query2, query3, keys_words, keys_s
             interleave(grouped[:], raw)
             banks.append(product(name, quantize(name, grouped, 1)[0], kw, ks))
         a, b, h = banks
-        dq_go = sb.tile([P, 2 * Q * PACK], BF16, name="dq_go", align_bytes=64)
+        vs = gather("vs", vs_pool, U8)
+        vw = gather("vw", vw_pool, U16)
+        dq_go = sb.tile([P, 2 * Q * PACK], BF16, name="dq_go", tag="before_max", align_bytes=64)
         interleave(dq_go[:, : Q * PACK], dq_raw)
         interleave(dq_go[:, Q * PACK :], go_raw)
+        dq_q, go_q = quantize("dq_go", dq_go, 2)
+        c0 = product("c0", go_q, vw, vs)
+        ta = product("ta", dq_q, kw, ks)
 
         size_ps = ps.tile([P, PACK, P], F32, name="size_ps")
         for j in range(PACK):
             nc.tensor.transpose(size_ps[:, j, :], size4[:, j : j + 1].to_broadcast([P, P]), ident[:])
+        size_row = wide("size_row")
+        nc.scalar.copy(size_row[:].rearrange("p (s j) -> p s j", j=PACK), size_ps[:].rearrange("p j s -> p s j"))
 
-        neg_maxes = []
+        neg_max3 = sb.tile([Q, 3], F32, name="neg_max3", tag="before_max", align_bytes=64)
         for n, bank in enumerate((a, b, h)):
-            part = sb.tile([Q, 1], F32, name="neg_max%d" % n, tag="after_max%d" % n, align_bytes=64)
-            nc.vector.tensor_reduce(part[:], bank[:], AX.X, ALU.max, negate=True)
-            neg_maxes.append(part)
-        neg_max = sb.tile([Q, 1], F32, name="neg_max", tag="after_exp", align_bytes=64)
-        nc.vector.tensor_scalar(neg_max[:], neg_maxes[0][:], neg_maxes[1][:], neg_maxes[2][:], ALU.min, ALU.min)
-
-        dq_q, go_q = quantize("dq_go", dq_go, 2, tag="after_max2")
-        ta = product("ta", dq_q, kw, ks)
-        vs = gather("vs", vs_pool, U8, tag="after_max0")
-        vw = gather("vw", vw_pool, U16, tag="after_max1")
-        c0 = product("c0", go_q, vw, vs)
+            nc.vector.tensor_reduce(neg_max3[:, n : n + 1], bank[:], AX.X, ALU.max, negate=True)
+        neg_max = column("neg_max")
+        nc.vector.tensor_reduce(neg_max[:], neg_max3[:], AX.X, ALU.min)
 
         z3 = column("z3", 3)
         exps = []
@@ -137,41 +134,35 @@ def tile_attend_hvcommittee_kernel(tc, query, query2, query3, keys_words, keys_s
             nc.scalar.activation(e[:], bank[:], ACT.Exp, bias=neg_max[:], accum_out=z3[:, n : n + 1])
             exps.append(e)
         ea, eb, eh = exps
-        z3n = column("z3n", 3)
-        neg_z = column("neg_z")
-        nc.scalar.activation(z3n[:], z3[:], ACT.Identity, scale=-1.0, accum_out=neg_z[:])
+        z3s = column("z3s", 3)
+        zs = column("zs")
+        nc.scalar.activation(z3s[:], z3[:], ACT.Identity, scale=OUT_SCALE, accum_out=zs[:])
 
-        size_row = sb.tile([Q, I], F32, name="size_row", tag="after_exp", align_bytes=64)
-        nc.scalar.copy(size_row[:].rearrange("p (s j) -> p s j", j=PACK), size_ps[:].rearrange("p j s -> p s j"))
-
-        x = late.tile([Q, I], F32, name="x", tag="vw_pool", align_bytes=64)
-        sum_x = column("sum_x")
-        nc.vector.scalar_tensor_tensor(x[:], ta[:], 1.0, ea[:], ALU.mult, ALU.mult, accum_out=sum_x[:])
         g = wide("g")
         nc.vector.tensor_tensor(g[:], c0[:], size_row[:], ALU.mult)
-        neg_rz = column("neg_rz")
-        nc.vector.reciprocal(neg_rz[:], neg_z[:])
+        x = wide("x")
+        sum_x = column("sum_x")
+        nc.vector.scalar_tensor_tensor(x[:], ta[:], -OUT_SCALE, ea[:], ALU.mult, ALU.mult, accum_out=sum_x[:])
+        dta = wide("dta")
+        nc.scalar.activation(dta[:], ta[:], ACT.Identity, scale=zs[:], bias=sum_x[:])
         t3 = column("t3", 3)
+        rzs = column("rzs")
         for n, e in enumerate(exps):
+            if n == 2:
+                nc.vector.reciprocal(rzs[:], zs[:])
             eg = wide("eg%d" % n)
-            nc.vector.scalar_tensor_tensor(eg[:], e[:], 1.0, g[:], ALU.mult, ALU.mult, accum_out=t3[:, n : n + 1])
+            nc.vector.scalar_tensor_tensor(eg[:], e[:], -OUT_SCALE, g[:], ALU.mult, ALU.mult, accum_out=t3[:, n : n + 1])
         xg = wide("xg")
         sum_xg = column("sum_xg")
         nc.vector.scalar_tensor_tensor(xg[:], x[:], 1.0, g[:], ALU.mult, ALU.mult, accum_out=sum_xg[:])
 
-        neg_xb = column("neg_xb")
-        nc.scalar.activation(neg_xb[:], sum_x[:], ACT.Identity, scale=neg_rz[:])
-        dta = wide("dta")
-        nc.scalar.activation(dta[:], ta[:], ACT.Identity, bias=neg_xb[:])
         k = column("k")
-        nc.scalar.activation(k[:], neg_rz[:], ACT.Identity, scale=-OUT_SCALE)
+        nc.scalar.activation(k[:], rzs[:], ACT.Square, scale=OUT_SCALE)
         t3n = column("t3n", 3)
         neg_mu = column("neg_mu")
-        nc.scalar.activation(t3n[:], t3[:], ACT.Identity, scale=neg_rz[:], accum_out=neg_mu[:])
-        xb_mu = column("xb_mu")
-        nc.scalar.activation(xb_mu[:], neg_mu[:], ACT.Identity, scale=neg_xb[:])
+        nc.scalar.activation(t3n[:], t3[:], ACT.Identity, scale=rzs[:], accum_out=neg_mu[:])
         neg_c = column("neg_c")
-        nc.scalar.activation(neg_c[:], sum_xg[:], ACT.Identity, scale=neg_rz[:], bias=xb_mu[:])
+        nc.scalar.activation(neg_c[:], neg_mu[:], ACT.Identity, scale=sum_x[:], bias=sum_xg[:])
 
         halves = [slice(0, I // 2), slice(I // 2, I)]
         u = [sb.tile([Q, I // 2], F32, name="u%d" % n, align_bytes=64) for n in range(2)]

@@ -35,8 +35,8 @@ def tile_attend_hvcommittee_kernel(tc, query, query2, query3, keys_words, keys_s
         def load_scale_rows(name, scales):
             plane = sb.tile([P, T], U8, name=name, align_bytes=64)
             nc.vector.memset(plane[:].bitcast(I32), 0)
-            for quad in range(4):
-                nc.sync.dma_start(plane[32 * quad : 32 * quad + 4, :].bitcast(I32), scales[0, 4 * quad : 4 * quad + 4, :].bitcast(I32))
+            for r in range(4):
+                nc.sync.dma_start(plane[r:P:32, :].bitcast(I32), scales[0, r:16:4, :].bitcast(I32))
             return plane
 
         def load_words(name, words):
@@ -45,7 +45,7 @@ def tile_attend_hvcommittee_kernel(tc, query, query2, query3, keys_words, keys_s
             return pool_words
 
         def load_rows(name, src):
-            raw = sb.tile([P, PACK * Q], F32, name=name, align_bytes=64)
+            raw = sb.tile([P, PACK * Q], F32, name=name, tag=name, align_bytes=64)
             nc.sync.dma_start(raw[:], src.rearrange("(p t) q -> p (t q)", t=PACK))
             return raw
 
@@ -78,6 +78,8 @@ def tile_attend_hvcommittee_kernel(tc, query, query2, query3, keys_words, keys_s
         def column(name, n=1):
             return sb.tile([Q, n], F32, name=name)
 
+        size4 = sb.tile([P, PACK], F32, name="size4")
+        nc.sync.dma_start(size4[:], size[0].rearrange("(p j) -> p j", j=PACK))
         kw_pool = load_words("kw_pool", keys_words)
         ks_pool = load_scale_rows("ks_pool", keys_scales)
         q1_raw = load_rows("q1_raw", query)
@@ -87,8 +89,6 @@ def tile_attend_hvcommittee_kernel(tc, query, query2, query3, keys_words, keys_s
         vw_pool = load_words("vw_pool", vals_words)
         dq_raw = load_rows("dq_raw", dquery)
         go_raw = load_rows("go_raw", gout)
-        size4 = sb.tile([P, PACK], F32, name="size4")
-        nc.sync.dma_start(size4[:], size[0].rearrange("(p j) -> p j", j=PACK))
         base_sb = wide("base_sb")
         nc.sync.dma_start(base_sb[:], base)
 
@@ -96,6 +96,12 @@ def tile_attend_hvcommittee_kernel(tc, query, query2, query3, keys_words, keys_s
         make_identity(nc, ident[:])
         warm = column("warm")
         nc.scalar.activation(warm[:], ident[:, 0:1], ACT.Exp)
+
+        size_ps = ps.tile([P, PACK, P], F32, name="size_ps")
+        for j in range(PACK):
+            nc.tensor.transpose(size_ps[:, j, :], size4[:, j : j + 1].to_broadcast([P, P]), ident[:])
+        size_row = wide("size_row")
+        nc.scalar.copy(size_row[:].rearrange("p (s j) -> p s j", j=PACK), size_ps[:].rearrange("p j s -> p s j"))
 
         kw = gather("kw", kw_pool, U16)
         ks = gather("ks", ks_pool, U8)
@@ -108,22 +114,17 @@ def tile_attend_hvcommittee_kernel(tc, query, query2, query3, keys_words, keys_s
         a, b, h = banks
         vs = gather("vs", vs_pool, U8)
         vw = gather("vw", vw_pool, U16)
-        dq_go = sb.tile([P, 2 * Q * PACK], BF16, name="dq_go", tag="before_max", align_bytes=64)
+        dq_go = sb.tile([P, 2 * Q * PACK], BF16, name="dq_go", align_bytes=64)
         interleave(dq_go[:, : Q * PACK], dq_raw)
         interleave(dq_go[:, Q * PACK :], go_raw)
+
+        neg_max3 = sb.tile([Q, 3], F32, name="neg_max3", tag="dq_raw", align_bytes=64)
+        for n, bank in enumerate((a, b)):
+            nc.vector.tensor_reduce(neg_max3[:, n : n + 1], bank[:], AX.X, ALU.max, negate=True)
         dq_q, go_q = quantize("dq_go", dq_go, 2)
         c0 = product("c0", go_q, vw, vs)
         ta = product("ta", dq_q, kw, ks)
-
-        size_ps = ps.tile([P, PACK, P], F32, name="size_ps")
-        for j in range(PACK):
-            nc.tensor.transpose(size_ps[:, j, :], size4[:, j : j + 1].to_broadcast([P, P]), ident[:])
-        size_row = wide("size_row")
-        nc.scalar.copy(size_row[:].rearrange("p (s j) -> p s j", j=PACK), size_ps[:].rearrange("p j s -> p s j"))
-
-        neg_max3 = sb.tile([Q, 3], F32, name="neg_max3", tag="before_max", align_bytes=64)
-        for n, bank in enumerate((a, b, h)):
-            nc.vector.tensor_reduce(neg_max3[:, n : n + 1], bank[:], AX.X, ALU.max, negate=True)
+        nc.vector.tensor_reduce(neg_max3[:, 2:3], h[:], AX.X, ALU.max, negate=True)
         neg_max = column("neg_max")
         nc.vector.tensor_reduce(neg_max[:], neg_max3[:], AX.X, ALU.min)
 
@@ -140,18 +141,22 @@ def tile_attend_hvcommittee_kernel(tc, query, query2, query3, keys_words, keys_s
 
         g = wide("g")
         nc.vector.tensor_tensor(g[:], c0[:], size_row[:], ALU.mult)
+        t3 = column("t3", 3)
+
+        def weighted_sum(n):
+            eg = wide("eg%d" % n)
+            nc.vector.scalar_tensor_tensor(eg[:], exps[n][:], -OUT_SCALE, g[:], ALU.mult, ALU.mult, accum_out=t3[:, n : n + 1])
+
+        weighted_sum(0)
         x = wide("x")
         sum_x = column("sum_x")
         nc.vector.scalar_tensor_tensor(x[:], ta[:], -OUT_SCALE, ea[:], ALU.mult, ALU.mult, accum_out=sum_x[:])
         dta = wide("dta")
         nc.scalar.activation(dta[:], ta[:], ACT.Identity, scale=zs[:], bias=sum_x[:])
-        t3 = column("t3", 3)
+        weighted_sum(1)
         rzs = column("rzs")
-        for n, e in enumerate(exps):
-            if n == 2:
-                nc.vector.reciprocal(rzs[:], zs[:])
-            eg = wide("eg%d" % n)
-            nc.vector.scalar_tensor_tensor(eg[:], e[:], -OUT_SCALE, g[:], ALU.mult, ALU.mult, accum_out=t3[:, n : n + 1])
+        nc.vector.reciprocal(rzs[:], zs[:])
+        weighted_sum(2)
         xg = wide("xg")
         sum_xg = column("sum_xg")
         nc.vector.scalar_tensor_tensor(xg[:], x[:], 1.0, g[:], ALU.mult, ALU.mult, accum_out=sum_xg[:])

@@ -56,8 +56,8 @@ def tile_attend_hvcommittee_kernel(tc, query, query2, query3, keys_words, keys_s
 
         def interleave(grouped, raw):
             nc.scalar.activation(
-                grouped.rearrange("p (q t) -> p q t", t=PACK),
-                raw[:].rearrange("p (t q) -> p q t", t=PACK),
+                grouped.rearrange("p (c i t) -> p c t i", i=4, t=PACK),
+                raw[:].rearrange("p (t c i) -> p c t i", i=4, t=PACK),
                 ACT.Copy,
             )
 
@@ -84,11 +84,11 @@ def tile_attend_hvcommittee_kernel(tc, query, query2, query3, keys_words, keys_s
         ks_pool = load_scale_rows("ks_pool", keys_scales)
         q1_raw = load_rows("q1_raw", query)
         q2_raw = load_rows("q2_raw", query2)
-        q3_raw = load_rows("q3_raw", query3)
         vs_pool = load_scale_rows("vs_pool", vals_scales)
+        q3_raw = load_rows("q3_raw", query3)
         vw_pool = load_words("vw_pool", vals_words)
-        dq_raw = load_rows("dq_raw", dquery)
         go_raw = load_rows("go_raw", gout)
+        dq_raw = load_rows("dq_raw", dquery)
         base_sb = wide("base_sb")
         nc.sync.dma_start(base_sb[:], base)
 
@@ -106,27 +106,28 @@ def tile_attend_hvcommittee_kernel(tc, query, query2, query3, keys_words, keys_s
         kw = gather("kw", kw_pool, U16)
         ks = gather("ks", ks_pool, U8)
 
-        banks = []
-        for name, raw in (("a", q1_raw), ("b", q2_raw), ("h", q3_raw)):
+        def scores(name, raw, words, scales):
             grouped = sb.tile([P, Q * PACK], BF16, name=name + "_bf", align_bytes=64)
             interleave(grouped[:], raw)
-            banks.append(product(name, quantize(name, grouped, 1)[0], kw, ks))
-        a, b, h = banks
-        vs = gather("vs", vs_pool, U8)
-        vw = gather("vw", vw_pool, U16)
-        dq_go = sb.tile([P, 2 * Q * PACK], BF16, name="dq_go", align_bytes=64)
-        interleave(dq_go[:, : Q * PACK], dq_raw)
-        interleave(dq_go[:, Q * PACK :], go_raw)
+            return product(name, quantize(name, grouped, 1)[0], words, scales)
 
-        neg_max3 = sb.tile([Q, 3], F32, name="neg_max3", tag="dq_raw", align_bytes=64)
-        for n, bank in enumerate((a, b)):
-            nc.vector.tensor_reduce(neg_max3[:, n : n + 1], bank[:], AX.X, ALU.max, negate=True)
-        dq_q, go_q = quantize("dq_go", dq_go, 2)
-        c0 = product("c0", go_q, vw, vs)
-        ta = product("ta", dq_q, kw, ks)
-        nc.vector.tensor_reduce(neg_max3[:, 2:3], h[:], AX.X, ALU.max, negate=True)
+        def negated_max(name, bank, slot):
+            part = sb.tile([Q, 1], F32, name=name, tag=slot, align_bytes=64)
+            nc.vector.tensor_reduce(part[:], bank[:], AX.X, ALU.max, negate=True)
+            return part
+
+        a = scores("a", q1_raw, kw, ks)
+        b = scores("b", q2_raw, kw, ks)
+        vs = gather("vs", vs_pool, U8)
+        h = scores("h", q3_raw, kw, ks)
+        neg_max_a = negated_max("neg_max_a", a, "q3_raw")
+        vw = gather("vw", vw_pool, U16)
+        c0 = scores("c0", go_raw, vw, vs)
+        neg_max_b = negated_max("neg_max_b", b, "go_raw")
+        ta = scores("ta", dq_raw, kw, ks)
+        neg_max_h = negated_max("neg_max_h", h, "dq_raw")
         neg_max = column("neg_max")
-        nc.vector.tensor_reduce(neg_max[:], neg_max3[:], AX.X, ALU.min)
+        nc.vector.tensor_scalar(neg_max[:], neg_max_h[:], neg_max_a[:], neg_max_b[:], ALU.min, ALU.min)
 
         z3 = column("z3", 3)
         exps = []

@@ -39,9 +39,9 @@ def tile_attend_hvcommittee_kernel(tc, query, query2, query3, keys_words, keys_s
                 nc.sync.dma_start(plane[r:P:32, :].bitcast(I32), scales[0, r:16:4, :].bitcast(I32))
             return plane
 
-        def load_words(name, words):
+        def load_words(name, words, queue):
             pool_words = sb.tile([P, T], U16, name=name, align_bytes=64)
-            nc.sync.dma_start(pool_words[:].bitcast(I32), words[0].bitcast(I32))
+            queue.dma_start(pool_words[:].bitcast(I32), words[0].bitcast(I32))
             return pool_words
 
         def load_rows(name, src):
@@ -80,13 +80,13 @@ def tile_attend_hvcommittee_kernel(tc, query, query2, query3, keys_words, keys_s
 
         size4 = sb.tile([P, PACK], F32, name="size4")
         nc.sync.dma_start(size4[:], size[0].rearrange("(p j) -> p j", j=PACK))
-        kw_pool = load_words("kw_pool", keys_words)
+        kw_pool = load_words("kw_pool", keys_words, nc.scalar)
         ks_pool = load_scale_rows("ks_pool", keys_scales)
         q1_raw = load_rows("q1_raw", query)
         q2_raw = load_rows("q2_raw", query2)
         vs_pool = load_scale_rows("vs_pool", vals_scales)
         q3_raw = load_rows("q3_raw", query3)
-        vw_pool = load_words("vw_pool", vals_words)
+        vw_pool = load_words("vw_pool", vals_words, nc.sync)
         go_raw = load_rows("go_raw", gout)
         dq_raw = load_rows("dq_raw", dquery)
         base_sb = wide("base_sb")
@@ -125,50 +125,66 @@ def tile_attend_hvcommittee_kernel(tc, query, query2, query3, keys_words, keys_s
         c0 = scores("c0", go_raw, vw, vs)
         neg_max_b = negated_max("neg_max_b", b, "go_raw")
         ta = scores("ta", dq_raw, kw, ks)
-        neg_max_h = negated_max("neg_max_h", h, "dq_raw")
-        neg_max = column("neg_max")
-        nc.vector.tensor_scalar(neg_max[:], neg_max_h[:], neg_max_a[:], neg_max_b[:], ALU.min, ALU.min)
+        ea_max = sb.tile([Q, I + 8], F32, name="ea_max", tag="dq_raw", align_bytes=64)
+        ea, neg_max_h = ea_max[:, :I], ea_max[:, I : I + 1]
+        nc.vector.tensor_reduce(neg_max_h, h[:], AX.X, ALU.max, negate=True)
+        neg_maxes = (neg_max_a[:], neg_max_b[:], neg_max_h)
 
         z3 = column("z3", 3)
-        exps = []
+        eb = wide("eb")
+        eh = wide("eh")
+        exps = (ea, eb[:], eh[:])
         for n, bank in enumerate((a, b, h)):
-            e = wide("exp%d" % n)
-            nc.scalar.activation(e[:], bank[:], ACT.Exp, bias=neg_max[:], accum_out=z3[:, n : n + 1])
-            exps.append(e)
-        ea, eb, eh = exps
-        z3s = column("z3s", 3)
-        zs = column("zs")
-        nc.scalar.activation(z3s[:], z3[:], ACT.Identity, scale=OUT_SCALE, accum_out=zs[:])
+            nc.scalar.activation(exps[n], bank[:], ACT.Exp, bias=neg_maxes[n], accum_out=z3[:, n : n + 1])
 
         g = wide("g")
         nc.vector.tensor_tensor(g[:], c0[:], size_row[:], ALU.mult)
+        neg_joint = column("neg_joint")
+        nc.vector.tensor_scalar(neg_joint[:], neg_max_h, neg_max_a[:], neg_max_b[:], ALU.min, ALU.min)
+        factors = []
+        for n in range(3):
+            f = column("factor%d" % n)
+            nc.scalar.activation(f[:], neg_maxes[n], ACT.Exp, scale=-1.0, bias=neg_joint[:])
+            factors.append(f)
+        zf3 = column("zf3", 3)
+        for n in range(3):
+            nc.scalar.activation(zf3[:, n : n + 1], z3[:, n : n + 1], ACT.Identity, scale=factors[n][:])
+        neg_zf3 = column("neg_zf3", 3)
+        neg_z = column("neg_z")
+        nc.scalar.activation(neg_zf3[:], zf3[:], ACT.Identity, scale=-1.0, accum_out=neg_z[:])
+
+        def weighted_sum(name, e, factor, total):
+            eg = wide(name)
+            nc.vector.scalar_tensor_tensor(eg[:], e, factor, g[:], ALU.mult, ALU.mult, accum_out=total)
+
         t3 = column("t3", 3)
-
-        def weighted_sum(n):
-            eg = wide("eg%d" % n)
-            nc.vector.scalar_tensor_tensor(eg[:], exps[n][:], -OUT_SCALE, g[:], ALU.mult, ALU.mult, accum_out=t3[:, n : n + 1])
-
-        weighted_sum(0)
+        t_a = column("t_a")
+        weighted_sum("eg_a", ea, 1.0, t_a[:])
         x = wide("x")
         sum_x = column("sum_x")
-        nc.vector.scalar_tensor_tensor(x[:], ta[:], -OUT_SCALE, ea[:], ALU.mult, ALU.mult, accum_out=sum_x[:])
+        nc.vector.scalar_tensor_tensor(x[:], ta[:], factors[0][:], ea, ALU.mult, ALU.mult, accum_out=sum_x[:])
         dta = wide("dta")
-        nc.scalar.activation(dta[:], ta[:], ACT.Identity, scale=zs[:], bias=sum_x[:])
-        weighted_sum(1)
-        rzs = column("rzs")
-        nc.vector.reciprocal(rzs[:], zs[:])
-        weighted_sum(2)
+        nc.scalar.activation(dta[:], ta[:], ACT.Identity, scale=neg_z[:], bias=sum_x[:])
+        nc.scalar.activation(t3[:, 0:1], t_a[:], ACT.Identity, scale=factors[0][:])
+        weighted_sum("eg_b", exps[1], factors[1][:], t3[:, 1:2])
+        neg_rz = column("neg_rz")
+        nc.vector.reciprocal(neg_rz[:], neg_z[:])
+        weighted_sum("eg_h", exps[2], factors[2][:], t3[:, 2:3])
         xg = wide("xg")
         sum_xg = column("sum_xg")
         nc.vector.scalar_tensor_tensor(xg[:], x[:], 1.0, g[:], ALU.mult, ALU.mult, accum_out=sum_xg[:])
 
-        k = column("k")
-        nc.scalar.activation(k[:], rzs[:], ACT.Square, scale=OUT_SCALE)
         t3n = column("t3n", 3)
         neg_mu = column("neg_mu")
-        nc.scalar.activation(t3n[:], t3[:], ACT.Identity, scale=rzs[:], accum_out=neg_mu[:])
+        nc.scalar.activation(t3n[:], t3[:], ACT.Identity, scale=neg_rz[:], accum_out=neg_mu[:])
         neg_c = column("neg_c")
         nc.scalar.activation(neg_c[:], neg_mu[:], ACT.Identity, scale=sum_x[:], bias=sum_xg[:])
+        out_factor = column("out_factor")
+        nc.scalar.activation(out_factor[:], factors[0][:], ACT.Identity, scale=-OUT_SCALE)
+        rz2 = column("rz2")
+        nc.scalar.activation(rz2[:], neg_rz[:], ACT.Square)
+        k = column("k")
+        nc.scalar.activation(k[:], rz2[:], ACT.Identity, scale=out_factor[:])
 
         halves = [slice(0, I // 2), slice(I // 2, I)]
         u = [sb.tile([Q, I // 2], F32, name="u%d" % n, align_bytes=64) for n in range(2)]
@@ -177,7 +193,7 @@ def tile_attend_hvcommittee_kernel(tc, query, query2, query3, keys_words, keys_s
         for n, cols in enumerate(halves):
             nc.vector.scalar_tensor_tensor(u[n][:], g[:, cols], neg_mu[:], dta[:, cols], ALU.add, ALU.mult)
         for n, cols in enumerate(halves):
-            nc.vector.scalar_tensor_tensor(v[n][:], u[n][:], neg_c[:], ea[:, cols], ALU.add, ALU.mult)
+            nc.vector.scalar_tensor_tensor(v[n][:], u[n][:], neg_c[:], ea_max[:, cols], ALU.add, ALU.mult)
         for n, cols in enumerate(halves):
             nc.vector.scalar_tensor_tensor(y[n][:], v[n][:], k[:], base_sb[:, cols], ALU.mult, ALU.add)
             nc.sync.dma_start(out[:, cols], y[n][:])

from contextlib import ExitStack

import concourse.mybir as mybir
from concourse.masks import make_identity

D, E, T, I, Q = 512, 512, 2048, 512, 128
FLOPS = 5 * 2 * D * Q * I

F32 = mybir.dt.float32
BF16 = mybir.dt.bfloat16
I32 = mybir.dt.int32
U32 = mybir.dt.uint32
U16 = mybir.dt.uint16
U8 = mybir.dt.uint8
FP8X4 = mybir.dt.float8_e4m3fn_x4
FP4X4 = mybir.dt.float4_e2m1fn_x4
ALU = mybir.AluOpType
ACT = mybir.ActivationFunctionType
AX = mybir.AxisListType

P = 128
PACK = 4
OUT_SCALE = 512.0


def tile_attend_hvcommittee_kernel(tc, query, query2, query3, keys_words, keys_scales, gout, vals_words, vals_scales, size, dquery, base, offs, out):
    nc = tc.nc
    with ExitStack() as ctx:
        sb = ctx.enter_context(tc.tile_pool(name="sb", bufs=1))
        ps = ctx.enter_context(tc.psum_pool(name="ps", bufs=1))

        offsets = sb.tile([P, I // 16], U16, name="offsets")
        nc.sync.dma_start(offsets[:], offs)

        def load_scale_rows(name, scales):
            plane = sb.tile([P, T], U8, name=name, align_bytes=64)
            nc.vector.memset(plane[:].bitcast(I32), 0)
            for r in range(4):
                nc.sync.dma_start(plane[r:P:32, :].bitcast(I32), scales[0, r:16:4, :].bitcast(I32))
            return plane

        def load_words(name, words, queue):
            pool_words = sb.tile([P, T], U16, name=name, align_bytes=64)
            queue.dma_start(pool_words[:].bitcast(I32), words[0].bitcast(I32))
            return pool_words

        def load_rows(name, src):
            raw = sb.tile([P, PACK * Q], F32, name=name, tag=name, align_bytes=64)
            nc.sync.dma_start(raw[:], src.rearrange("(p t) q -> p (t q)", t=PACK))
            return raw

        def gather(name, window, dtype):
            picked = sb.tile([P, I], dtype, name=name, align_bytes=64)
            nc.vector.tensor_copy(picked[:], window[:].indirect(offsets[:]))
            return picked

        def interleave(grouped, raw):
            nc.scalar.activation(
                grouped.rearrange("p (c i t) -> p c t i", i=4, t=PACK),
                raw[:].rearrange("p (t c i) -> p c t i", i=4, t=PACK),
                ACT.Copy,
            )

        def quantize(name, grouped, n):
            codes = sb.tile([P, n * Q], U32, name=name + "_codes", align_bytes=64)
            scales = sb.tile([P, n * Q], U8, name=name + "_scales", align_bytes=64)
            nc.vector.quantize_mx(out=codes[:].bitcast(FP8X4), scales=scales[:], in_=grouped[:])
            return [(codes[:, m * Q : (m + 1) * Q], scales[:, m * Q : (m + 1) * Q]) for m in range(n)]

        def product(name, rows, words, scales):
            bank = ps.tile([Q, I], F32, name=name)
            nc.tensor.matmul_mx(out=bank[:], lhsT=rows[0].bitcast(FP8X4), lhsT_scale=rows[1], rhs=words[:].bitcast(FP4X4), rhs_scale=scales[:], start=True, stop=True)
            return bank

        def wide(name):
            return sb.tile([Q, I], F32, name=name, align_bytes=64)

        def column(name, n=1):
            return sb.tile([Q, n], F32, name=name)

        size4 = sb.tile([P, PACK], F32, name="size4")
        nc.sync.dma_start(size4[:], size[0].rearrange("(p j) -> p j", j=PACK))
        kw_pool = load_words("kw_pool", keys_words, nc.scalar)
        ks_pool = load_scale_rows("ks_pool", keys_scales)
        q1_raw = load_rows("q1_raw", query)
        q2_raw = load_rows("q2_raw", query2)
        vs_pool = load_scale_rows("vs_pool", vals_scales)
        q3_raw = load_rows("q3_raw", query3)
        vw_pool = load_words("vw_pool", vals_words, nc.sync)
        go_raw = load_rows("go_raw", gout)
        dq_raw = load_rows("dq_raw", dquery)
        base_sb = wide("base_sb")
        nc.sync.dma_start(base_sb[:], base)

        ident = sb.tile([P, P], F32, name="ident")
        make_identity(nc, ident[:])
        warm = column("warm")
        nc.scalar.activation(warm[:], ident[:, 0:1], ACT.Exp)

        size_ps = ps.tile([P, PACK, P], F32, name="size_ps")
        for j in range(PACK):
            nc.tensor.transpose(size_ps[:, j, :], size4[:, j : j + 1].to_broadcast([P, P]), ident[:])
        size_row = wide("size_row")
        nc.scalar.copy(size_row[:].rearrange("p (s j) -> p s j", j=PACK), size_ps[:].rearrange("p j s -> p s j"))

        kw = gather("kw", kw_pool, U16)
        ks = gather("ks", ks_pool, U8)

        def scores(name, raw, words, scales):
            grouped = sb.tile([P, Q * PACK], BF16, name=name + "_bf", align_bytes=64)
            interleave(grouped[:], raw)
            return product(name, quantize(name, grouped, 1)[0], words, scales)

        def negated_max(name, bank, slot):
            part = sb.tile([Q, 1], F32, name=name, tag=slot, align_bytes=64)
            nc.vector.tensor_reduce(part[:], bank[:], AX.X, ALU.max, negate=True)
            return part

        a = scores("a", q1_raw, kw, ks)
        b = scores("b", q2_raw, kw, ks)
        vs = gather("vs", vs_pool, U8)
        h = scores("h", q3_raw, kw, ks)
        neg_max_a = negated_max("neg_max_a", a, "q3_raw")
        vw = gather("vw", vw_pool, U16)
        c0 = scores("c0", go_raw, vw, vs)
        neg_max_b = negated_max("neg_max_b", b, "go_raw")
        ta = scores("ta", dq_raw, kw, ks)
        ea_max = sb.tile([Q, I + 8], F32, name="ea_max", tag="dq_raw", align_bytes=64)
        ea, neg_max_h = ea_max[:, :I], ea_max[:, I : I + 1]
        nc.vector.tensor_reduce(neg_max_h, h[:], AX.X, ALU.max, negate=True)
        neg_maxes = (neg_max_a[:], neg_max_b[:], neg_max_h)

        z3 = column("z3", 3)
        eb = wide("eb")
        eh = wide("eh")
        exps = (ea, eb[:], eh[:])
        for n, bank in enumerate((a, b, h)):
            nc.scalar.activation(exps[n], bank[:], ACT.Exp, bias=neg_maxes[n], accum_out=z3[:, n : n + 1])

        g = wide("g")
        nc.vector.tensor_tensor(g[:], c0[:], size_row[:], ALU.mult)
        neg_joint = column("neg_joint")
        nc.vector.tensor_scalar(neg_joint[:], neg_max_h, neg_max_a[:], neg_max_b[:], ALU.min, ALU.min)
        factors = []
        for n in range(3):
            f = column("factor%d" % n)
            nc.scalar.activation(f[:], neg_maxes[n], ACT.Exp, scale=-1.0, bias=neg_joint[:])
            factors.append(f)
        zf3 = column("zf3", 3)
        for n in range(3):
            nc.scalar.activation(zf3[:, n : n + 1], z3[:, n : n + 1], ACT.Identity, scale=factors[n][:])
        neg_zf3 = column("neg_zf3", 3)
        neg_z = column("neg_z")
        nc.scalar.activation(neg_zf3[:], zf3[:], ACT.Identity, scale=-1.0, accum_out=neg_z[:])

        def weighted_sum(name, e, factor, total):
            eg = wide(name)
            nc.vector.scalar_tensor_tensor(eg[:], e, factor, g[:], ALU.mult, ALU.mult, accum_out=total)

        t3 = column("t3", 3)
        t_a = column("t_a")
        weighted_sum("eg_a", ea, 1.0, t_a[:])
        x = wide("x")
        sum_x = column("sum_x")
        nc.vector.scalar_tensor_tensor(x[:], ta[:], factors[0][:], ea, ALU.mult, ALU.mult, accum_out=sum_x[:])
        dta = wide("dta")
        nc.scalar.activation(dta[:], ta[:], ACT.Identity, scale=neg_z[:], bias=sum_x[:])
        nc.scalar.activation(t3[:, 0:1], t_a[:], ACT.Identity, scale=factors[0][:])
        weighted_sum("eg_b", exps[1], factors[1][:], t3[:, 1:2])
        neg_rz = column("neg_rz")
        nc.vector.reciprocal(neg_rz[:], neg_z[:])
        weighted_sum("eg_h", exps[2], factors[2][:], t3[:, 2:3])
        xg = wide("xg")
        sum_xg = column("sum_xg")
        nc.vector.scalar_tensor_tensor(xg[:], x[:], 1.0, g[:], ALU.mult, ALU.mult, accum_out=sum_xg[:])

        t3n = column("t3n", 3)
        neg_mu = column("neg_mu")
        nc.scalar.activation(t3n[:], t3[:], ACT.Identity, scale=neg_rz[:], accum_out=neg_mu[:])
        neg_c = column("neg_c")
        nc.scalar.activation(neg_c[:], neg_mu[:], ACT.Identity, scale=sum_x[:], bias=sum_xg[:])
        out_factor = column("out_factor")
        nc.scalar.activation(out_factor[:], factors[0][:], ACT.Identity, scale=-OUT_SCALE)
        rz2 = column("rz2")
        nc.scalar.activation(rz2[:], neg_rz[:], ACT.Square)
        k = column("k")
        nc.scalar.activation(k[:], rz2[:], ACT.Identity, scale=out_factor[:])

        halves = [slice(0, I // 2), slice(I // 2, I)]
        u = [sb.tile([Q, I // 2], F32, name="u%d" % n, align_bytes=64) for n in range(2)]
        v = [sb.tile([Q, I // 2], F32, name="v%d" % n, align_bytes=64) for n in range(2)]
        y = [sb.tile([Q, I // 2], F32, name="y%d" % n, align_bytes=64) for n in range(2)]
        for n, cols in enumerate(halves):
            nc.vector.scalar_tensor_tensor(u[n][:], g[:, cols], neg_mu[:], dta[:, cols], ALU.add, ALU.mult)
        for n, cols in enumerate(halves):
            nc.vector.scalar_tensor_tensor(v[n][:], u[n][:], neg_c[:], ea_max[:, cols], ALU.add, ALU.mult)
        for n, cols in enumerate(halves):
            nc.vector.scalar_tensor_tensor(y[n][:], v[n][:], k[:], base_sb[:, cols], ALU.mult, ALU.add)
            nc.sync.dma_start(out[:, cols], y[n][:])
